import numpy as np
import ml_dtypes


def mxq(x, axis, fmt="e4m3"):
    dtype, down = {"e4m3": (ml_dtypes.float8_e4m3fn, 7), "e5m2": (ml_dtypes.float8_e5m2, 14)}[fmt]
    v = np.moveaxis(np.asarray(x, np.float32).astype(ml_dtypes.bfloat16).astype(np.float64), axis, -1)
    blocks = v.reshape(v.shape[:-1] + (-1, 32))
    amax = np.abs(blocks).max(-1, keepdims=True)
    byte = np.maximum(np.where(amax > 0, np.frexp(amax)[1] - 1 + 127, 0) - down, 1)
    scale = np.exp2(byte - 127.0)
    codes = (blocks / scale).astype(np.float32).astype(dtype).astype(np.float64)
    return np.moveaxis((codes * scale).reshape(v.shape), -1, axis)


WIDE = False


def mx_kscale(k):
    if not WIDE:
        return np.ones(k)
    levels = np.array([10, -10, 5, -5, 0])
    if k % 512:
        return np.exp2(np.random.permutation(np.resize(levels, k // 32))).repeat(32)
    a = np.empty((k // 512, 16))
    for p in range(k // 512):
        a[p, :8] = np.random.permutation(np.resize(levels, 8))
        for g in range(8):
            far = levels[np.abs(levels - a[p, g]) >= 10]
            a[p, g + 8] = far[np.random.randint(len(far))]
    return np.exp2(a.ravel()).repeat(32)


def f64(x):
    return np.asarray(x).astype(np.float64)


def striped(idx):
    return np.tile(idx.reshape(-1, 16).T, (8, 1)).astype(np.uint16)


def unstriped(offs):
    return offs[:16].T.reshape(-1).astype(np.int64)


def pack_weight(w):
    k, n = w.shape
    w = f64(np.asarray(w, np.float32).astype(ml_dtypes.bfloat16)).reshape(k // 32, 32, n)
    amax = np.abs(w).max(1)
    byte = np.clip(np.where(amax > 0, np.frexp(amax)[1] - 1 + 127 - 7, 1), 1, 254)
    scaled = (w * np.exp2(127.0 - byte)[:, None, :]).reshape(k, n).astype(np.float32)
    words = np.ascontiguousarray(scaled.reshape(k // 512, 128, 4, n).transpose(0, 1, 3, 2)).astype(ml_dtypes.float8_e4m3fn).view(np.uint8)
    return words, np.ascontiguousarray(byte.astype(np.uint8).reshape(k // 512, 16, n))


def unpack_weight(words, scales):
    g, p, n, _ = words.shape
    vals = np.ascontiguousarray(words).view(ml_dtypes.float8_e4m3fn).astype(np.float64) * np.repeat(np.exp2(scales.astype(np.float64) - 127.0), 8, axis=1)[..., None]
    return vals.transpose(0, 1, 3, 2).reshape(g * 512, n)


K, T, E, C, N = 1024, 512, 4, 256, 512


def by_expert(wq, xq):
    return np.concatenate([wq[e].T @ xq[:, e * C:(e + 1) * C] for e in range(E)], axis=1)


def setup_inputs():
    n = np.random.standard_normal
    s = mx_kscale(K)[:, None]
    first = np.random.permutation(np.repeat(np.arange(E), T // E))
    second = (first + 1 + np.random.permutation(np.repeat(np.arange(E - 1), -(-T // (E - 1)))[:T])) % E
    while np.bincount(second, minlength=E).max() != T // E:
        load = np.bincount(second, minlength=E); hi, lo = int(load.argmax()), int(load.argmin())
        t = np.flatnonzero((second == hi) & (first != lo))[0]; second[t] = lo
    slot_token = np.empty(E * C, np.int64); pos = np.empty((2, T), np.int64); fill = np.zeros(E, np.int64)
    place = np.stack([np.random.permutation(C) for _ in range(E)])
    for r, deal in enumerate((first, second)):
        for t in np.random.permutation(T):
            e = deal[t]; j = e * C + place[e, fill[e]]; fill[e] += 1; slot_token[j] = t; pos[r, t] = j
    g = np.random.uniform(0.2, 0.8, T)
    packed = [pack_weight(m) for m in n((E, K, N)) / np.sqrt(K) / s[None]]
    return {
        "xT": (n((K, T)) * s).astype(np.float32),
        "w_words": np.stack([m[0] for m in packed]),
        "w_scales": np.stack([m[1] for m in packed]),
        "gate": np.stack([np.tile(g, (N, 1)), np.tile(1.0 - g, (N, 1))]).astype(np.float32),
        "offs": striped(slot_token),
        "pos1": striped(pos[0]),
        "pos2": striped(pos[1]),
    }


def reference(xT, w_words, w_scales, gate, offs, pos1, pos2):
    idx = unstriped(offs)
    xq = mxq(f64(xT)[:, idx], 0, "e4m3")
    w = np.stack([unpack_weight(w_words[e], w_scales[e]) for e in range(E)])
    y = by_expert(w, xq)
    return f64(gate[0]) * y[:, unstriped(pos1)] + f64(gate[1]) * y[:, unstriped(pos2)]

@@ -1,0 +1,185 @@
+from contextlib import ExitStack
+
+import concourse.mybir as mybir
+from concourse.masks import make_identity
+
+K, T, E, C, N = 1024, 512, 4, 256, 512
+FLOPS = 2 * K * N * E * C
+
+F32 = mybir.dt.float32
+BF16 = mybir.dt.bfloat16
+I32 = mybir.dt.int32
+U32 = mybir.dt.uint32
+U16 = mybir.dt.uint16
+U8 = mybir.dt.uint8
+FP8X4 = mybir.dt.float8_e4m3fn_x4
+MULT = mybir.AluOpType.mult
+ADD = mybir.AluOpType.add
+
+P = 128
+PACK = 4
+PASSES = K // (P * PACK)
+NB = N // P
+WINDOW = (1536, 512)
+HALF = T // 2
+VSHARE = 176
+PE_SUMS = 3
+
+
+def tile_routed_moe_kernel(tc, xT, w_words, w_scales, gate, offs, pos1, pos2, out):
+    nc = tc.nc
+    with ExitStack() as ctx:
+        lists = ctx.enter_context(tc.tile_pool(name="lists", bufs=1))
+        keep = ctx.enter_context(tc.tile_pool(name="keep", bufs=1))
+        work = ctx.enter_context(tc.tile_pool(name="work", bufs=3))
+        psum = ctx.enter_context(tc.psum_pool(name="psum", bufs=1))
+
+        offs_t = lists.tile([P, E * C // 16], U16, name="offs_t")
+        pos1_t = lists.tile([P, T // 16], U16, name="pos1_t")
+        pos2_t = lists.tile([P, T // 16], U16, name="pos2_t")
+
+        raw = [keep.tile([P, PACK, T], F32, name="raw%d" % a) for a in range(PASSES)]
+        grouped = [keep.tile([P, T, PACK], BF16, name="grouped%d" % a, align_bytes=64) for a in range(PASSES)]
+        tok_codes = [keep.tile([P, WINDOW[a]], I32, name="tok_codes%d" % a, align_bytes=64) for a in range(PASSES)]
+        tok_scales = keep.tile([P, T], U8, name="tok_scales", align_bytes=64)
+        slot_codes = keep.tile([P, PASSES, E * C], U32, name="slot_codes", align_bytes=64)
+        slot_scales = keep.tile([P, E * C], U8, name="slot_scales", align_bytes=64)
+        w_codes = keep.tile([P, E * PASSES, N], I32, name="w_codes", align_bytes=64)
+        w_planes = keep.tile([P, E * PASSES, N], U8, name="w_planes", align_bytes=64)
+        gates = [keep.tile([P, 2, T], F32, name="gates%d" % nb) for nb in range(NB)]
+        y = [keep.tile([P, E * C], F32, name="y%d" % nb) for nb in range(NB)]
+        acc = [[psum.tile([P, 2 * C], F32, name="acc%d_%d" % (nb, h)) for h in range(2)] for nb in range(NB)]
+
+        nc.vector.memset(w_planes[:].rearrange("p g n -> p (g n)").bitcast(I32), 0)
+        nc.vector.memset(tok_scales[:].bitcast(I32), 0)
+        nc.vector.memset(tok_codes[0][:, T:], 0)
+
+        x_view = xT.rearrange("(a p j) w -> a p j w", p=P, j=PACK)
+        for h in range(2):
+            nc.sync.dma_start(raw[0][:, :, h * HALF:(h + 1) * HALF], x_view[0][:, :, h * HALF:(h + 1) * HALF])
+        nc.sync.dma_start(offs_t[:], offs)
+        for h in range(2):
+            nc.sync.dma_start(raw[1][:, :, h * HALF:(h + 1) * HALF], x_view[1][:, :, h * HALF:(h + 1) * HALF])
+        s_view = w_scales.rearrange("e a (q r) n -> r q (e a) n", r=4)
+        for r in range(4):
+            nc.sync.dma_start(w_planes[r:P:32, :, :].bitcast(I32), s_view[r].bitcast(I32))
+        for e in range(E):
+            nc.sync.dma_start(
+                w_codes[:, e * PASSES:(e + 1) * PASSES, :],
+                w_words[e].rearrange("a p n r -> p a (n r)").bitcast(I32),
+            )
+        nc.sync.dma_start(pos1_t[:], pos1)
+        nc.sync.dma_start(pos2_t[:], pos2)
+        for nb in range(NB):
+            nc.sync.dma_start(gates[nb][:], gate[:, nb * P:(nb + 1) * P, :].rearrange("r p t -> p r t"))
+
+        def interleave(engine_copy, a, t0, t1):
+            engine_copy(
+                out=grouped[a][:, t0:t1, :].rearrange("p (c i) j -> p c j i", i=4),
+                in_=raw[a][:, :, t0:t1].rearrange("p j (c i) -> p c j i", i=4),
+            )
+
+        def quantise(a, t0, t1):
+            nc.vector.quantize_mx(
+                out=tok_codes[a][:, t0:t1].bitcast(FP8X4),
+                scales=tok_scales[4 * a:P, t0:t1],
+                in_=grouped[a][:, t0:t1, :].rearrange("p w j -> p (w j)"),
+            )
+
+        def fetch_codes(a, e0, e1):
+            nc.vector.tensor_copy(
+                out=slot_codes[:, a, e0 * C:e1 * C],
+                in_=tok_codes[a][:].bitcast(U32).indirect(offs_t[:, e0 * C // 16:e1 * C // 16]),
+            )
+
+        def fetch_scales(e0, e1):
+            nc.vector.tensor_copy(
+                out=slot_scales[:, e0 * C:e1 * C],
+                in_=tok_scales[:].indirect(offs_t[:, e0 * C // 16:e1 * C // 16]),
+            )
+
+        def bank(nb, e):
+            return acc[nb][e % 2][:, (e // 2) * C:(e // 2 + 1) * C]
+
+        def multiply(a, e, nb):
+            cols = slice(e * C, (e + 1) * C)
+            feats = slice(nb * P, (nb + 1) * P)
+            nc.tensor.matmul_mx(
+                out=bank(nb, e),
+                lhsT=w_codes[:, e * PASSES + a, feats].bitcast(FP8X4),
+                lhsT_scale=w_planes[:, e * PASSES + a, feats],
+                rhs=slot_codes[:, a, cols].bitcast(FP8X4),
+                rhs_scale=slot_scales[4 * a:P, cols],
+                start=(a == 0),
+                stop=(a == PASSES - 1),
+            )
+
+        def evict(e, nb):
+            engine_copy = nc.vector.tensor_copy if (e, nb) == (E - 1, 0) else nc.scalar.copy
+            engine_copy(out=y[nb][:, e * C:(e + 1) * C], in_=bank(nb, e))
+
+        def evict_pair(h, nb):
+            nc.scalar.copy(
+                out=y[nb][:].rearrange("p (g h c) -> p h g c", g=2, h=2)[:, h],
+                in_=acc[nb][h][:].rearrange("p (g c) -> p g c", g=2),
+            )
+
+        ident = keep.tile([P, P], F32, name="ident")
+        make_identity(nc, ident[:])
+
+        for h in range(2):
+            interleave(nc.vector.tensor_copy, 0, h * HALF, h * HALF + VSHARE)
+            interleave(nc.scalar.copy, 0, h * HALF + VSHARE, (h + 1) * HALF)
+            quantise(0, h * HALF, (h + 1) * HALF)
+        interleave(nc.scalar.copy, 1, 0, HALF)
+        interleave(nc.scalar.copy, 1, HALF, T)
+
+        fetch_codes(0, 0, E)
+        for h in range(2):
+            quantise(1, h * HALF, (h + 1) * HALF)
+        for e in range(E):
+            if e < E - 1:
+                fetch_scales(e, e + 1)
+                for nb in range(NB):
+                    multiply(0, e, nb)
+                fetch_codes(1, e, e + 1)
+                for nb in range(NB):
+                    multiply(1, e, nb)
+            else:
+                fetch_codes(1, e, e + 1)
+                fetch_scales(e, e + 1)
+                for nb in range(NB):
+                    for a in range(PASSES):
+                        multiply(a, e, nb)
+            evict(e, 0)
+            if e >= 2:
+                for nb in range(1, NB):
+                    evict_pair(e - 2, nb)
+
+        for nb in range(PE_SUMS):
+            first = work.tile([P, T], F32, name="first")
+            second = work.tile([P, T], F32, name="second")
+            total = work.tile([P, T], F32, name="total")
+            nc.vector.tensor_tensor(out=first[:], in0=y[nb][:].indirect(pos1_t[:]), in1=gates[nb][:, 0, :], op=MULT)
+            nc.vector.tensor_tensor(out=second[:], in0=y[nb][:].indirect(pos2_t[:]), in1=gates[nb][:, 1, :], op=MULT)
+            both = psum.tile([P, T], F32, name="acc%d_0" % nb)
+            nc.tensor.matmul(both[:], lhsT=ident[:], rhs=first[:], start=True, stop=False)
+            nc.tensor.matmul(both[:], lhsT=ident[:], rhs=second[:], start=False, stop=True)
+            nc.scalar.copy(out=total[:], in_=both[:])
+            nc.sync.dma_start(out[nb * P:(nb + 1) * P, :], total[:])
+
+        nb = NB - 1
+        first = work.tile([P, T], F32, name="first")
+        second = work.tile([P, T], F32, name="second")
+        total = work.tile([P, T], F32, name="total")
+        nc.vector.tensor_tensor(out=first[:], in0=y[nb][:].indirect(pos1_t[:]), in1=gates[nb][:, 0, :], op=MULT)
+        for h in range(2):
+            cols = slice(h * HALF, (h + 1) * HALF)
+            nc.vector.tensor_tensor(
+                out=second[:, cols],
+                in0=y[nb][:].indirect(pos2_t[:, h * HALF // 16:(h + 1) * HALF // 16]),
+                in1=gates[nb][:, 1, cols],
+                op=MULT,
+            )
+            nc.vector.tensor_tensor(out=total[:, cols], in0=first[:, cols], in1=second[:, cols], op=ADD)
+            nc.sync.dma_start(out[nb * P:(nb + 1) * P, cols], total[:, cols])

@@ -48,7 +48,8 @@ def tile_routed_moe_kernel(tc, xT, w_words, w_scales, gate, offs, pos1, pos2, ou
         w_planes = keep.tile([P, E * PASSES, N], U8, name="w_planes", align_bytes=64)
         gates = [keep.tile([P, 2, T], F32, name="gates%d" % nb) for nb in range(NB)]
         y = [keep.tile([P, E * C], F32, name="y%d" % nb) for nb in range(NB)]
-        acc = [[psum.tile([P, 2 * C], F32, name="acc%d_%d" % (nb, h)) for h in range(2)] for nb in range(NB)]
+        acc = [[psum.tile([P, 2 * C], F32, name="acc%d_%d" % (nb, h)) for h in range(2)] for nb in range(NB - 1)]
+        acc.append([None, None])
 
         nc.vector.memset(w_planes[:].rearrange("p g n -> p (g n)").bitcast(I32), 0)
         nc.vector.memset(tok_scales[:].bitcast(I32), 0)
@@ -140,21 +141,29 @@ def tile_routed_moe_kernel(tc, xT, w_words, w_scales, gate, offs, pos1, pos2, ou
         for e in range(E):
             if e < E - 1:
                 fetch_scales(e, e + 1)
-                for nb in range(NB):
+                for nb in range(NB - 1):
                     multiply(0, e, nb)
                 fetch_codes(1, e, e + 1)
-                for nb in range(NB):
+                for nb in range(NB - 1):
                     multiply(1, e, nb)
             else:
                 fetch_codes(1, e, e + 1)
                 fetch_scales(e, e + 1)
-                for nb in range(NB):
+                for nb in range(NB - 1):
                     for a in range(PASSES):
                         multiply(a, e, nb)
             evict(e, 0)
             if e >= 2:
-                for nb in range(1, NB):
+                for nb in range(1, NB - 1):
                     evict_pair(e - 2, nb)
+
+        for h in range(2):
+            late = psum.tile([P, 2 * C], F32, name="acc%d_1" % h)
+            acc[NB - 1][h] = late
+            for e in (h, h + 2):
+                for a in range(PASSES):
+                    multiply(a, e, NB - 1)
+            evict_pair(h, NB - 1)
 
         for nb in range(PE_SUMS):
             first = work.tile([P, T], F32, name="first")
@@ -162,7 +171,7 @@ def tile_routed_moe_kernel(tc, xT, w_words, w_scales, gate, offs, pos1, pos2, ou
             total = work.tile([P, T], F32, name="total")
             nc.vector.tensor_tensor(out=first[:], in0=y[nb][:].indirect(pos1_t[:]), in1=gates[nb][:, 0, :], op=MULT)
             nc.vector.tensor_tensor(out=second[:], in0=y[nb][:].indirect(pos2_t[:]), in1=gates[nb][:, 1, :], op=MULT)
-            both = psum.tile([P, T], F32, name="acc%d_0" % nb)
+            both = psum.tile([P, T], F32, name="sum%d" % (nb % 2))
             nc.tensor.matmul(both[:], lhsT=ident[:], rhs=first[:], start=True, stop=False)
             nc.tensor.matmul(both[:], lhsT=ident[:], rhs=second[:], start=False, stop=True)
             nc.scalar.copy(out=total[:], in_=both[:])

@@ -100,7 +100,9 @@ def tile_routed_moe_kernel(tc, xT, w_words, w_scales, gate, offs, pos1, pos2, ou
             )
 
         def bank(nb, e):
-            return acc[nb][e % 2][:, (e // 2) * C:(e // 2 + 1) * C]
+            if nb == 0:
+                return acc[nb][e % 2][:, (e // 2) * C:(e // 2 + 1) * C]
+            return acc[nb][e // 2][:, (e % 2) * C:(e % 2 + 1) * C]
 
         def multiply(a, e, nb):
             cols = slice(e * C, (e + 1) * C)
@@ -116,14 +118,10 @@ def tile_routed_moe_kernel(tc, xT, w_words, w_scales, gate, offs, pos1, pos2, ou
             )
 
         def evict(e, nb):
-            engine_copy = nc.vector.tensor_copy if (e, nb) == (E - 1, 0) else nc.scalar.copy
-            engine_copy(out=y[nb][:, e * C:(e + 1) * C], in_=bank(nb, e))
+            nc.scalar.copy(out=y[nb][:, e * C:(e + 1) * C], in_=bank(nb, e))
 
         def evict_pair(h, nb):
-            nc.scalar.copy(
-                out=y[nb][:].rearrange("p (g h c) -> p h g c", g=2, h=2)[:, h],
-                in_=acc[nb][h][:].rearrange("p (g c) -> p g c", g=2),
-            )
+            nc.scalar.copy(out=y[nb][:, h * 2 * C:(h + 1) * 2 * C], in_=acc[nb][h][:])
 
         ident = keep.tile([P, P], F32, name="ident")
         make_identity(nc, ident[:])
@@ -139,28 +137,21 @@ def tile_routed_moe_kernel(tc, xT, w_words, w_scales, gate, offs, pos1, pos2, ou
         for h in range(2):
             quantise(1, h * HALF, (h + 1) * HALF)
         for e in range(E):
-            if e < E - 1:
-                fetch_scales(e, e + 1)
-                for nb in range(NB - 1):
-                    multiply(0, e, nb)
-                fetch_codes(1, e, e + 1)
-                for nb in range(NB - 1):
-                    multiply(1, e, nb)
-            else:
-                fetch_codes(1, e, e + 1)
-                fetch_scales(e, e + 1)
-                for nb in range(NB - 1):
-                    for a in range(PASSES):
-                        multiply(a, e, nb)
+            fetch_scales(e, e + 1)
+            for nb in range(NB - 1):
+                multiply(0, e, nb)
+            fetch_codes(1, e, e + 1)
+            for nb in range(NB - 1):
+                multiply(1, e, nb)
             evict(e, 0)
-            if e >= 2:
+            if e % 2 == 1:
                 for nb in range(1, NB - 1):
-                    evict_pair(e - 2, nb)
+                    evict_pair(e // 2, nb)
 
         for h in range(2):
             late = psum.tile([P, 2 * C], F32, name="acc%d_1" % h)
             acc[NB - 1][h] = late
-            for e in (h, h + 2):
+            for e in (2 * h, 2 * h + 1):
                 for a in range(PASSES):
                     multiply(a, e, NB - 1)
             evict_pair(h, NB - 1)

@@ -50,6 +50,7 @@ def tile_routed_moe_kernel(tc, xT, w_words, w_scales, gate, offs, pos1, pos2, ou
         y = [keep.tile([P, E * C], F32, name="y%d" % nb) for nb in range(NB)]
         acc = [[psum.tile([P, 2 * C], F32, name="acc%d_%d" % (nb, h)) for h in range(2)] for nb in range(NB - 1)]
         acc.append([None, None])
+        spare = psum.tile([P, 2 * C], F32, name="sum1")
 
         nc.vector.memset(w_planes[:].rearrange("p g n -> p (g n)").bitcast(I32), 0)
         nc.vector.memset(tok_scales[:].bitcast(I32), 0)
@@ -87,11 +88,14 @@ def tile_routed_moe_kernel(tc, xT, w_words, w_scales, gate, offs, pos1, pos2, ou
                 in_=grouped[a][:, t0:t1, :].rearrange("p w j -> p (w j)"),
             )
 
-        def fetch_codes(a, e0, e1):
+        def fetch_code_slots(a, s0, s1):
             nc.vector.tensor_copy(
-                out=slot_codes[:, a, e0 * C:e1 * C],
-                in_=tok_codes[a][:].bitcast(U32).indirect(offs_t[:, e0 * C // 16:e1 * C // 16]),
+                out=slot_codes[:, a, s0:s1],
+                in_=tok_codes[a][:].bitcast(U32).indirect(offs_t[:, s0 // 16:s1 // 16]),
             )
+
+        def fetch_codes(a, e0, e1):
+            fetch_code_slots(a, e0 * C, e1 * C)
 
         def fetch_scales(e0, e1):
             nc.vector.tensor_copy(
@@ -104,11 +108,16 @@ def tile_routed_moe_kernel(tc, xT, w_words, w_scales, gate, offs, pos1, pos2, ou
                 return acc[nb][e % 2][:, (e // 2) * C:(e // 2 + 1) * C]
             return acc[nb][e // 2][:, (e % 2) * C:(e % 2 + 1) * C]
 
-        def multiply(a, e, nb):
-            cols = slice(e * C, (e + 1) * C)
+        def part(nb, e, c0, c1):
+            if (nb, e, c0) == (0, E - 1, C // 2):
+                return spare[:, c0:c1]
+            return bank(nb, e)[:, c0:c1]
+
+        def multiply(a, e, nb, c0=0, c1=C):
+            cols = slice(e * C + c0, e * C + c1)
             feats = slice(nb * P, (nb + 1) * P)
             nc.tensor.matmul_mx(
-                out=bank(nb, e),
+                out=part(nb, e, c0, c1),
                 lhsT=w_codes[:, e * PASSES + a, feats].bitcast(FP8X4),
                 lhsT_scale=w_planes[:, e * PASSES + a, feats],
                 rhs=slot_codes[:, a, cols].bitcast(FP8X4),
@@ -117,8 +126,8 @@ def tile_routed_moe_kernel(tc, xT, w_words, w_scales, gate, offs, pos1, pos2, ou
                 stop=(a == PASSES - 1),
             )
 
-        def evict(e, nb):
-            nc.scalar.copy(out=y[nb][:, e * C:(e + 1) * C], in_=bank(nb, e))
+        def evict(e, nb, c0=0, c1=C):
+            nc.scalar.copy(out=y[nb][:, e * C + c0:e * C + c1], in_=part(nb, e, c0, c1))
 
         def evict_pair(h, nb):
             nc.scalar.copy(out=y[nb][:, h * 2 * C:(h + 1) * 2 * C], in_=acc[nb][h][:])
@@ -136,7 +145,7 @@ def tile_routed_moe_kernel(tc, xT, w_words, w_scales, gate, offs, pos1, pos2, ou
         fetch_codes(0, 0, E)
         for h in range(2):
             quantise(1, h * HALF, (h + 1) * HALF)
-        for e in range(E):
+        for e in range(E - 1):
             fetch_scales(e, e + 1)
             for nb in range(NB - 1):
                 multiply(0, e, nb)
@@ -147,6 +156,20 @@ def tile_routed_moe_kernel(tc, xT, w_words, w_scales, gate, offs, pos1, pos2, ou
             if e % 2 == 1:
                 for nb in range(1, NB - 1):
                     evict_pair(e // 2, nb)
+
+        e = E - 1
+        fetch_scales(e, e + 1)
+        for c0 in (0, C // 2):
+            multiply(0, e, 0, c0, c0 + C // 2)
+        for nb in range(1, NB - 1):
+            multiply(0, e, nb)
+        for c0 in (0, C // 2):
+            fetch_code_slots(1, e * C + c0, e * C + c0 + C // 2)
+            multiply(1, e, 0, c0, c0 + C // 2)
+            evict(e, 0, c0, c0 + C // 2)
+        for nb in range(1, NB - 1):
+            multiply(1, e, nb)
+            evict_pair(e // 2, nb)
 
         for h in range(2):
             late = psum.tile([P, 2 * C], F32, name="acc%d_1" % h)

@@ -23,6 +23,7 @@ NB = N // P
 WINDOW = (1536, 512)
 HALF = T // 2
 VSHARE = 176
+EARLY = 2
 PE_SUMS = 3
 
 
@@ -48,8 +49,8 @@ def tile_routed_moe_kernel(tc, xT, w_words, w_scales, gate, offs, pos1, pos2, ou
         w_planes = keep.tile([P, E * PASSES, N], U8, name="w_planes", align_bytes=64)
         gates = [keep.tile([P, 2, T], F32, name="gates%d" % nb) for nb in range(NB)]
         y = [keep.tile([P, E * C], F32, name="y%d" % nb) for nb in range(NB)]
-        acc = [[psum.tile([P, 2 * C], F32, name="acc%d_%d" % (nb, h)) for h in range(2)] for nb in range(NB - 1)]
-        acc.append([None, None])
+        acc = [[psum.tile([P, 2 * C], F32, name="acc%d_%d" % (nb, h)) for h in range(2)] for nb in range(EARLY)]
+        acc.extend([[None, None] for nb in range(EARLY, NB)])
         spare = psum.tile([P, 2 * C], F32, name="sum1")
 
         nc.vector.memset(w_planes[:].rearrange("p g n -> p (g n)").bitcast(I32), 0)
@@ -147,37 +148,38 @@ def tile_routed_moe_kernel(tc, xT, w_words, w_scales, gate, offs, pos1, pos2, ou
             quantise(1, h * HALF, (h + 1) * HALF)
         for e in range(E - 1):
             fetch_scales(e, e + 1)
-            for nb in range(NB - 1):
+            for nb in range(EARLY):
                 multiply(0, e, nb)
             fetch_codes(1, e, e + 1)
-            for nb in range(NB - 1):
+            for nb in range(EARLY):
                 multiply(1, e, nb)
             evict(e, 0)
             if e % 2 == 1:
-                for nb in range(1, NB - 1):
+                for nb in range(1, EARLY):
                     evict_pair(e // 2, nb)
 
         e = E - 1
         fetch_scales(e, e + 1)
         for c0 in (0, C // 2):
             multiply(0, e, 0, c0, c0 + C // 2)
-        for nb in range(1, NB - 1):
+        for nb in range(1, EARLY):
             multiply(0, e, nb)
         for c0 in (0, C // 2):
             fetch_code_slots(1, e * C + c0, e * C + c0 + C // 2)
             multiply(1, e, 0, c0, c0 + C // 2)
             evict(e, 0, c0, c0 + C // 2)
-        for nb in range(1, NB - 1):
+        for nb in range(1, EARLY):
             multiply(1, e, nb)
             evict_pair(e // 2, nb)
 
-        for h in range(2):
-            late = psum.tile([P, 2 * C], F32, name="acc%d_1" % h)
-            acc[NB - 1][h] = late
-            for e in (2 * h, 2 * h + 1):
-                for a in range(PASSES):
-                    multiply(a, e, NB - 1)
-            evict_pair(h, NB - 1)
+        for nb in range(EARLY, NB):
+            for h in range(2):
+                late = psum.tile([P, 2 * C], F32, name="acc%d_1" % h)
+                acc[nb][h] = late
+                for e in (2 * h, 2 * h + 1):
+                    for a in range(PASSES):
+                        multiply(a, e, nb)
+                evict_pair(h, nb)
 
         for nb in range(PE_SUMS):
             first = work.tile([P, T], F32, name="first")
@@ -185,7 +187,7 @@ def tile_routed_moe_kernel(tc, xT, w_words, w_scales, gate, offs, pos1, pos2, ou
             total = work.tile([P, T], F32, name="total")
             nc.vector.tensor_tensor(out=first[:], in0=y[nb][:].indirect(pos1_t[:]), in1=gates[nb][:, 0, :], op=MULT)
             nc.vector.tensor_tensor(out=second[:], in0=y[nb][:].indirect(pos2_t[:]), in1=gates[nb][:, 1, :], op=MULT)
-            both = psum.tile([P, T], F32, name="sum%d" % (nb % 2))
+            both = psum.tile([P, T], F32, name="sum%d" % nb)
             nc.tensor.matmul(both[:], lhsT=ident[:], rhs=first[:], start=True, stop=False)
             nc.tensor.matmul(both[:], lhsT=ident[:], rhs=second[:], start=False, stop=True)
             nc.scalar.copy(out=total[:], in_=both[:])

@@ -23,6 +23,7 @@ NB = N // P
 WINDOW = (1536, 512)
 HALF = T // 2
 VSHARE = 176
+VSHARE1 = 48
 EARLY = 2
 PE_SUMS = 3
 
@@ -141,9 +142,10 @@ def tile_routed_moe_kernel(tc, xT, w_words, w_scales, gate, offs, pos1, pos2, ou
             interleave(nc.scalar.copy, 0, h * HALF + VSHARE, (h + 1) * HALF)
             quantise(0, h * HALF, (h + 1) * HALF)
         interleave(nc.scalar.copy, 1, 0, HALF)
-        interleave(nc.scalar.copy, 1, HALF, T)
+        interleave(nc.scalar.copy, 1, HALF, T - VSHARE1)
 
         fetch_codes(0, 0, E)
+        interleave(nc.vector.tensor_copy, 1, T - VSHARE1, T)
         for h in range(2):
             quantise(1, h * HALF, (h + 1) * HALF)
         for e in range(E - 1):

@@ -23,7 +23,7 @@ NB = N // P
 WINDOW = (1536, 512)
 HALF = T // 2
 VSHARE = 176
-VSHARE1 = 48
+VSHARE1 = 96
 EARLY = 2
 PE_SUMS = 3
 

@@ -21,6 +21,7 @@ PACK = 4
 PASSES = K // (P * PACK)
 NB = N // P
 WINDOW = (1536, 512)
+SCALE_WINDOW = 768
 HALF = T // 2
 VSHARE = 176
 VSHARE1 = 96
@@ -43,7 +44,7 @@ def tile_routed_moe_kernel(tc, xT, w_words, w_scales, gate, offs, pos1, pos2, ou
         raw = [keep.tile([P, PACK, T], F32, name="raw%d" % a) for a in range(PASSES)]
         grouped = [keep.tile([P, T, PACK], BF16, name="grouped%d" % a, align_bytes=64) for a in range(PASSES)]
         tok_codes = [keep.tile([P, WINDOW[a]], I32, name="tok_codes%d" % a, align_bytes=64) for a in range(PASSES)]
-        tok_scales = keep.tile([P, T], U8, name="tok_scales", align_bytes=64)
+        tok_scales = keep.tile([P, SCALE_WINDOW], U8, name="tok_scales", align_bytes=64)
         slot_codes = keep.tile([P, PASSES, E * C], U32, name="slot_codes", align_bytes=64)
         slot_scales = keep.tile([P, E * C], U8, name="slot_scales", align_bytes=64)
         w_codes = keep.tile([P, E * PASSES, N], I32, name="w_codes", align_bytes=64)
@@ -148,31 +149,25 @@ def tile_routed_moe_kernel(tc, xT, w_words, w_scales, gate, offs, pos1, pos2, ou
         interleave(nc.vector.tensor_copy, 1, T - VSHARE1, T)
         for h in range(2):
             quantise(1, h * HALF, (h + 1) * HALF)
-        for e in range(E - 1):
-            fetch_scales(e, e + 1)
-            for nb in range(EARLY):
-                multiply(0, e, nb)
-            fetch_codes(1, e, e + 1)
-            for nb in range(EARLY):
-                multiply(1, e, nb)
-            evict(e, 0)
-            if e % 2 == 1:
-                for nb in range(1, EARLY):
-                    evict_pair(e // 2, nb)
+        def pieces(e):
+            return ((0, C // 2), (C // 2, C)) if e == E - 1 else ((0, C),)
 
-        e = E - 1
-        fetch_scales(e, e + 1)
-        for c0 in (0, C // 2):
-            multiply(0, e, 0, c0, c0 + C // 2)
-        for nb in range(1, EARLY):
-            multiply(0, e, nb)
-        for c0 in (0, C // 2):
-            fetch_code_slots(1, e * C + c0, e * C + c0 + C // 2)
-            multiply(1, e, 0, c0, c0 + C // 2)
-            evict(e, 0, c0, c0 + C // 2)
-        for nb in range(1, EARLY):
-            multiply(1, e, nb)
-            evict_pair(e // 2, nb)
+        for e in range(E):
+            if e % 2 == 0:
+                fetch_scales(e, e + 2)
+                for ee in (e, e + 1):
+                    for c0, c1 in pieces(ee):
+                        multiply(0, ee, 0, c0, c1)
+            for nb in range(1, EARLY):
+                multiply(0, e, nb)
+            for c0, c1 in pieces(e):
+                fetch_code_slots(1, e * C + c0, e * C + c1)
+                multiply(1, e, 0, c0, c1)
+                evict(e, 0, c0, c1)
+            for nb in range(1, EARLY):
+                multiply(1, e, nb)
+                if e % 2 == 1:
+                    evict_pair(e // 2, nb)
 
         for nb in range(EARLY, NB):
             for h in range(2):

@@ -23,7 +23,7 @@ NB = N // P
 WINDOW = (1536, 512)
 SCALE_WINDOW = 768
 HALF = T // 2
-VSHARE = 176
+VSHARE = 208
 VSHARE1 = 96
 EARLY = 2
 PE_SUMS = 3

@@ -23,7 +23,7 @@ NB = N // P
 WINDOW = (1536, 512)
 SCALE_WINDOW = 768
 HALF = T // 2
-VSHARE = 208
+VSHARE = 176
 VSHARE1 = 96
 EARLY = 2
 PE_SUMS = 3
@@ -60,8 +60,7 @@ def tile_routed_moe_kernel(tc, xT, w_words, w_scales, gate, offs, pos1, pos2, ou
         nc.vector.memset(tok_codes[0][:, T:], 0)
 
         x_view = xT.rearrange("(a p j) w -> a p j w", p=P, j=PACK)
-        for h in range(2):
-            nc.sync.dma_start(raw[0][:, :, h * HALF:(h + 1) * HALF], x_view[0][:, :, h * HALF:(h + 1) * HALF])
+        nc.sync.dma_start(raw[0][:], x_view[0])
         nc.sync.dma_start(offs_t[:], offs)
         for h in range(2):
             nc.sync.dma_start(raw[1][:, :, h * HALF:(h + 1) * HALF], x_view[1][:, :, h * HALF:(h + 1) * HALF])

@@ -23,8 +23,7 @@ NB = N // P
 WINDOW = (1536, 512)
 SCALE_WINDOW = 768
 HALF = T // 2
-VSHARE = 176
-VSHARE1 = 96
+VSHARE = 144
 EARLY = 2
 PE_SUMS = 3
 
@@ -142,10 +141,9 @@ def tile_routed_moe_kernel(tc, xT, w_words, w_scales, gate, offs, pos1, pos2, ou
             interleave(nc.scalar.copy, 0, h * HALF + VSHARE, (h + 1) * HALF)
             quantise(0, h * HALF, (h + 1) * HALF)
         interleave(nc.scalar.copy, 1, 0, HALF)
-        interleave(nc.scalar.copy, 1, HALF, T - VSHARE1)
+        interleave(nc.scalar.copy, 1, HALF, T)
 
         fetch_codes(0, 0, E)
-        interleave(nc.vector.tensor_copy, 1, T - VSHARE1, T)
         for h in range(2):
             quantise(1, h * HALF, (h + 1) * HALF)
         def pieces(e):

@@ -23,7 +23,8 @@ NB = N // P
 WINDOW = (1536, 512)
 SCALE_WINDOW = 768
 HALF = T // 2
-VSHARE = 144
+VSHARE0 = 336
+VSHARE = 160
 EARLY = 2
 PE_SUMS = 3
 
@@ -59,7 +60,8 @@ def tile_routed_moe_kernel(tc, xT, w_words, w_scales, gate, offs, pos1, pos2, ou
         nc.vector.memset(tok_codes[0][:, T:], 0)
 
         x_view = xT.rearrange("(a p j) w -> a p j w", p=P, j=PACK)
-        nc.sync.dma_start(raw[0][:], x_view[0])
+        for j0 in range(0, PACK, 2):
+            nc.sync.dma_start(raw[0][:, j0:j0 + 2, :], x_view[0][:, j0:j0 + 2, :])
         nc.sync.dma_start(offs_t[:], offs)
         for h in range(2):
             nc.sync.dma_start(raw[1][:, :, h * HALF:(h + 1) * HALF], x_view[1][:, :, h * HALF:(h + 1) * HALF])
@@ -76,10 +78,10 @@ def tile_routed_moe_kernel(tc, xT, w_words, w_scales, gate, offs, pos1, pos2, ou
         for nb in range(NB):
             nc.sync.dma_start(gates[nb][:], gate[:, nb * P:(nb + 1) * P, :].rearrange("r p t -> p r t"))
 
-        def interleave(engine_copy, a, t0, t1):
+        def interleave(engine_copy, a, t0, t1, j0=0, j1=PACK):
             engine_copy(
-                out=grouped[a][:, t0:t1, :].rearrange("p (c i) j -> p c j i", i=4),
-                in_=raw[a][:, :, t0:t1].rearrange("p j (c i) -> p c j i", i=4),
+                out=grouped[a][:, t0:t1, j0:j1].rearrange("p (c i) j -> p c j i", i=4),
+                in_=raw[a][:, j0:j1, t0:t1].rearrange("p j (c i) -> p c j i", i=4),
             )
 
         def quantise(a, t0, t1):
@@ -136,9 +138,11 @@ def tile_routed_moe_kernel(tc, xT, w_words, w_scales, gate, offs, pos1, pos2, ou
         ident = keep.tile([P, P], F32, name="ident")
         make_identity(nc, ident[:])
 
+        interleave(nc.vector.tensor_copy, 0, 0, VSHARE0, 0, 2)
+        interleave(nc.scalar.copy, 0, VSHARE0, T, 0, 2)
         for h in range(2):
-            interleave(nc.vector.tensor_copy, 0, h * HALF, h * HALF + VSHARE)
-            interleave(nc.scalar.copy, 0, h * HALF + VSHARE, (h + 1) * HALF)
+            interleave(nc.vector.tensor_copy, 0, h * HALF, h * HALF + VSHARE, 2, PACK)
+            interleave(nc.scalar.copy, 0, h * HALF + VSHARE, (h + 1) * HALF, 2, PACK)
             quantise(0, h * HALF, (h + 1) * HALF)
         interleave(nc.scalar.copy, 1, 0, HALF)
         interleave(nc.scalar.copy, 1, HALF, T)

@@ -53,7 +53,7 @@ def tile_routed_moe_kernel(tc, xT, w_words, w_scales, gate, offs, pos1, pos2, ou
         y = [keep.tile([P, E * C], F32, name="y%d" % nb) for nb in range(NB)]
         acc = [[psum.tile([P, 2 * C], F32, name="acc%d_%d" % (nb, h)) for h in range(2)] for nb in range(EARLY)]
         acc.extend([[None, None] for nb in range(EARLY, NB)])
-        spare = psum.tile([P, 2 * C], F32, name="sum1")
+        spare = psum.tile([P, 2 * C], F32, name="spare")
 
         nc.vector.memset(w_planes[:].rearrange("p g n -> p (g n)").bitcast(I32), 0)
         nc.vector.memset(tok_scales[:].bitcast(I32), 0)
@@ -170,9 +170,10 @@ def tile_routed_moe_kernel(tc, xT, w_words, w_scales, gate, offs, pos1, pos2, ou
                 if e % 2 == 1:
                     evict_pair(e // 2, nb)
 
+        late_banks = {(2, 0): "acc0_1", (2, 1): "spare", (3, 0): "acc1_1", (3, 1): "acc0_1"}
         for nb in range(EARLY, NB):
             for h in range(2):
-                late = psum.tile([P, 2 * C], F32, name="acc%d_1" % h)
+                late = psum.tile([P, 2 * C], F32, name=late_banks[nb, h])
                 acc[nb][h] = late
                 for e in (2 * h, 2 * h + 1):
                     for a in range(PASSES):

from contextlib import ExitStack

import concourse.mybir as mybir
from concourse.masks import make_identity

K, T, E, C, N = 1024, 512, 4, 256, 512
FLOPS = 2 * K * N * E * C

F32 = mybir.dt.float32
BF16 = mybir.dt.bfloat16
I32 = mybir.dt.int32
U32 = mybir.dt.uint32
U16 = mybir.dt.uint16
U8 = mybir.dt.uint8
FP8X4 = mybir.dt.float8_e4m3fn_x4
MULT = mybir.AluOpType.mult
ADD = mybir.AluOpType.add

P = 128
PACK = 4
PASSES = K // (P * PACK)
NB = N // P
WINDOW = (1536, 512)
SCALE_WINDOW = 768
HALF = T // 2
VSHARE0 = 336
VSHARE = 160
EARLY = 2
PE_SUMS = 3


def tile_routed_moe_kernel(tc, xT, w_words, w_scales, gate, offs, pos1, pos2, out):
    nc = tc.nc
    with ExitStack() as ctx:
        lists = ctx.enter_context(tc.tile_pool(name="lists", bufs=1))
        keep = ctx.enter_context(tc.tile_pool(name="keep", bufs=1))
        work = ctx.enter_context(tc.tile_pool(name="work", bufs=3))
        psum = ctx.enter_context(tc.psum_pool(name="psum", bufs=1))

        offs_t = lists.tile([P, E * C // 16], U16, name="offs_t")
        pos1_t = lists.tile([P, T // 16], U16, name="pos1_t")
        pos2_t = lists.tile([P, T // 16], U16, name="pos2_t")

        raw = [keep.tile([P, PACK, T], F32, name="raw%d" % a) for a in range(PASSES)]
        grouped = [keep.tile([P, T, PACK], BF16, name="grouped%d" % a, align_bytes=64) for a in range(PASSES)]
        tok_codes = [keep.tile([P, WINDOW[a]], I32, name="tok_codes%d" % a, align_bytes=64) for a in range(PASSES)]
        tok_scales = keep.tile([P, SCALE_WINDOW], U8, name="tok_scales", align_bytes=64)
        slot_codes = keep.tile([P, PASSES, E * C], U32, name="slot_codes", align_bytes=64)
        slot_scales = keep.tile([P, E * C], U8, name="slot_scales", align_bytes=64)
        w_codes = keep.tile([P, E * PASSES, N], I32, name="w_codes", align_bytes=64)
        w_planes = keep.tile([P, E * PASSES, N], U8, name="w_planes", align_bytes=64)
        gates = [keep.tile([P, 2, T], F32, name="gates%d" % nb) for nb in range(NB)]
        y = [keep.tile([P, E * C], F32, name="y%d" % nb) for nb in range(NB)]
        acc = [[psum.tile([P, 2 * C], F32, name="acc%d_%d" % (nb, h)) for h in range(2)] for nb in range(EARLY)]
        acc.extend([[None, None] for nb in range(EARLY, NB)])
        spare = psum.tile([P, 2 * C], F32, name="spare")

        nc.vector.memset(w_planes[:].rearrange("p g n -> p (g n)").bitcast(I32), 0)
        nc.vector.memset(tok_scales[:].bitcast(I32), 0)
        nc.vector.memset(tok_codes[0][:, T:], 0)

        x_view = xT.rearrange("(a p j) w -> a p j w", p=P, j=PACK)
        for j0 in range(0, PACK, 2):
            nc.sync.dma_start(raw[0][:, j0:j0 + 2, :], x_view[0][:, j0:j0 + 2, :])
        nc.sync.dma_start(offs_t[:], offs)
        for h in range(2):
            nc.sync.dma_start(raw[1][:, :, h * HALF:(h + 1) * HALF], x_view[1][:, :, h * HALF:(h + 1) * HALF])
        s_view = w_scales.rearrange("e a (q r) n -> r q (e a) n", r=4)
        for r in range(4):
            nc.sync.dma_start(w_planes[r:P:32, :, :].bitcast(I32), s_view[r].bitcast(I32))
        for e in range(E):
            nc.sync.dma_start(
                w_codes[:, e * PASSES:(e + 1) * PASSES, :],
                w_words[e].rearrange("a p n r -> p a (n r)").bitcast(I32),
            )
        nc.sync.dma_start(pos1_t[:], pos1)
        nc.sync.dma_start(pos2_t[:], pos2)
        for nb in range(NB):
            nc.sync.dma_start(gates[nb][:], gate[:, nb * P:(nb + 1) * P, :].rearrange("r p t -> p r t"))

        def interleave(engine_copy, a, t0, t1, j0=0, j1=PACK):
            engine_copy(
                out=grouped[a][:, t0:t1, j0:j1].rearrange("p (c i) j -> p c j i", i=4),
                in_=raw[a][:, j0:j1, t0:t1].rearrange("p j (c i) -> p c j i", i=4),
            )

        def quantise(a, t0, t1):
            nc.vector.quantize_mx(
                out=tok_codes[a][:, t0:t1].bitcast(FP8X4),
                scales=tok_scales[4 * a:P, t0:t1],
                in_=grouped[a][:, t0:t1, :].rearrange("p w j -> p (w j)"),
            )

        def fetch_code_slots(a, s0, s1):
            nc.vector.tensor_copy(
                out=slot_codes[:, a, s0:s1],
                in_=tok_codes[a][:].bitcast(U32).indirect(offs_t[:, s0 // 16:s1 // 16]),
            )

        def fetch_codes(a, e0, e1):
            fetch_code_slots(a, e0 * C, e1 * C)

        def fetch_scales(e0, e1):
            nc.vector.tensor_copy(
                out=slot_scales[:, e0 * C:e1 * C],
                in_=tok_scales[:].indirect(offs_t[:, e0 * C // 16:e1 * C // 16]),
            )

        def bank(nb, e):
            if nb == 0:
                return acc[nb][e % 2][:, (e // 2) * C:(e // 2 + 1) * C]
            return acc[nb][e // 2][:, (e % 2) * C:(e % 2 + 1) * C]

        def part(nb, e, c0, c1):
            if (nb, e, c0) == (0, E - 1, C // 2):
                return spare[:, c0:c1]
            return bank(nb, e)[:, c0:c1]

        def multiply(a, e, nb, c0=0, c1=C):
            cols = slice(e * C + c0, e * C + c1)
            feats = slice(nb * P, (nb + 1) * P)
            nc.tensor.matmul_mx(
                out=part(nb, e, c0, c1),
                lhsT=w_codes[:, e * PASSES + a, feats].bitcast(FP8X4),
                lhsT_scale=w_planes[:, e * PASSES + a, feats],
                rhs=slot_codes[:, a, cols].bitcast(FP8X4),
                rhs_scale=slot_scales[4 * a:P, cols],
                start=(a == 0),
                stop=(a == PASSES - 1),
            )

        def evict(e, nb, c0=0, c1=C):
            nc.scalar.copy(out=y[nb][:, e * C + c0:e * C + c1], in_=part(nb, e, c0, c1))

        def evict_pair(h, nb):
            nc.scalar.copy(out=y[nb][:, h * 2 * C:(h + 1) * 2 * C], in_=acc[nb][h][:])

        ident = keep.tile([P, P], F32, name="ident")
        make_identity(nc, ident[:])

        interleave(nc.vector.tensor_copy, 0, 0, VSHARE0, 0, 2)
        interleave(nc.scalar.copy, 0, VSHARE0, T, 0, 2)
        for h in range(2):
            interleave(nc.vector.tensor_copy, 0, h * HALF, h * HALF + VSHARE, 2, PACK)
            interleave(nc.scalar.copy, 0, h * HALF + VSHARE, (h + 1) * HALF, 2, PACK)
            quantise(0, h * HALF, (h + 1) * HALF)
        interleave(nc.scalar.copy, 1, 0, HALF)
        interleave(nc.scalar.copy, 1, HALF, T)

        fetch_codes(0, 0, E)
        for h in range(2):
            quantise(1, h * HALF, (h + 1) * HALF)
        def pieces(e):
            return ((0, C // 2), (C // 2, C)) if e == E - 1 else ((0, C),)

        for e in range(E):
            if e % 2 == 0:
                fetch_scales(e, e + 2)
                for ee in (e, e + 1):
                    for c0, c1 in pieces(ee):
                        multiply(0, ee, 0, c0, c1)
            for nb in range(1, EARLY):
                multiply(0, e, nb)
            for c0, c1 in pieces(e):
                fetch_code_slots(1, e * C + c0, e * C + c1)
                multiply(1, e, 0, c0, c1)
                evict(e, 0, c0, c1)
            for nb in range(1, EARLY):
                multiply(1, e, nb)
                if e % 2 == 1:
                    evict_pair(e // 2, nb)

        late_banks = {(2, 0): "acc0_1", (2, 1): "spare", (3, 0): "acc1_1", (3, 1): "acc0_1"}
        for nb in range(EARLY, NB):
            for h in range(2):
                late = psum.tile([P, 2 * C], F32, name=late_banks[nb, h])
                acc[nb][h] = late
                for e in (2 * h, 2 * h + 1):
                    for a in range(PASSES):
                        multiply(a, e, nb)
                evict_pair(h, nb)

        for nb in range(PE_SUMS):
            first = work.tile([P, T], F32, name="first")
            second = work.tile([P, T], F32, name="second")
            total = work.tile([P, T], F32, name="total")
            nc.vector.tensor_tensor(out=first[:], in0=y[nb][:].indirect(pos1_t[:]), in1=gates[nb][:, 0, :], op=MULT)
            nc.vector.tensor_tensor(out=second[:], in0=y[nb][:].indirect(pos2_t[:]), in1=gates[nb][:, 1, :], op=MULT)
            both = psum.tile([P, T], F32, name="sum%d" % nb)
            nc.tensor.matmul(both[:], lhsT=ident[:], rhs=first[:], start=True, stop=False)
            nc.tensor.matmul(both[:], lhsT=ident[:], rhs=second[:], start=False, stop=True)
            nc.scalar.copy(out=total[:], in_=both[:])
            nc.sync.dma_start(out[nb * P:(nb + 1) * P, :], total[:])

        nb = NB - 1
        first = work.tile([P, T], F32, name="first")
        second = work.tile([P, T], F32, name="second")
        total = work.tile([P, T], F32, name="total")
        nc.vector.tensor_tensor(out=first[:], in0=y[nb][:].indirect(pos1_t[:]), in1=gates[nb][:, 0, :], op=MULT)
        for h in range(2):
            cols = slice(h * HALF, (h + 1) * HALF)
            nc.vector.tensor_tensor(
                out=second[:, cols],
                in0=y[nb][:].indirect(pos2_t[:, h * HALF // 16:(h + 1) * HALF // 16]),
                in1=gates[nb][:, 1, cols],
                op=MULT,
            )
            nc.vector.tensor_tensor(out=total[:, cols], in0=first[:, cols], in1=second[:, cols], op=ADD)
            nc.sync.dma_start(out[nb * P:(nb + 1) * P, cols], total[:, cols])
